import numpy as np
import ml_dtypes


def mxq(x, axis, fmt="e4m3"):
    dtype, down = {"e4m3": (ml_dtypes.float8_e4m3fn, 7), "e5m2": (ml_dtypes.float8_e5m2, 14)}[fmt]
    v = np.moveaxis(np.asarray(x, np.float32).astype(ml_dtypes.bfloat16).astype(np.float64), axis, -1)
    blocks = v.reshape(v.shape[:-1] + (-1, 32))
    amax = np.abs(blocks).max(-1, keepdims=True)
    byte = np.maximum(np.where(amax > 0, np.frexp(amax)[1] - 1 + 127, 0) - down, 1)
    scale = np.exp2(byte - 127.0)
    codes = (blocks / scale).astype(np.float32).astype(dtype).astype(np.float64)
    return np.moveaxis((codes * scale).reshape(v.shape), -1, axis)


WIDE = False


def mx_kscale(k):
    if not WIDE:
        return np.ones(k)
    levels = np.array([10, -10, 5, -5, 0])
    if k % 512:
        return np.exp2(np.random.permutation(np.resize(levels, k // 32))).repeat(32)
    a = np.empty((k // 512, 16))
    for p in range(k // 512):
        a[p, :8] = np.random.permutation(np.resize(levels, 8))
        for g in range(8):
            far = levels[np.abs(levels - a[p, g]) >= 10]
            a[p, g + 8] = far[np.random.randint(len(far))]
    return np.exp2(a.ravel()).repeat(32)


def f64(x):
    return np.asarray(x).astype(np.float64)


def striped(idx):
    return np.tile(idx.reshape(-1, 16).T, (8, 1)).astype(np.uint16)


def unstriped(offs):
    return offs[:16].T.reshape(-1).astype(np.int64)


E2M1 = np.array([0.0, 0.5, 1.0, 1.5, 2.0, 3.0, 4.0, 6.0, -0.0, -0.5, -1.0, -1.5, -2.0, -3.0, -4.0, -6.0])


def pack_weight(w, fmt):
    k, n = w.shape
    w = f64(np.asarray(w, np.float32).astype(ml_dtypes.bfloat16)).reshape(k // 32, 32, n)
    amax = np.abs(w).max(1)
    if fmt == "e4m3":
        byte = np.frexp(amax)[1] - 1 + 127 - 7
    else:
        mant, ex = np.frexp(amax / 6.0)
        byte = np.where(mant > 0.5, ex, ex - 1) + 127
    byte = np.clip(np.where(amax > 0, byte, 1), 1, 254)
    scaled = (w * np.exp2(127.0 - byte)[:, None, :]).reshape(k, n).astype(np.float32)
    by_word = np.ascontiguousarray(scaled.reshape(k // 512, 128, 4, n).transpose(0, 1, 3, 2))
    if fmt == "e4m3":
        words = by_word.astype(ml_dtypes.float8_e4m3fn).view(np.uint8)
    else:
        c = by_word.astype(ml_dtypes.float4_e2m1fn).view(np.uint8) & 0xF
        words = (c[..., 0::2] | (c[..., 1::2] << 4)).reshape(k // 512, 128, 2 * n)
    return np.ascontiguousarray(words), np.ascontiguousarray(byte.astype(np.uint8).reshape(k // 512, 16, n))


def unpack_weight(words, scales, fmt):
    g, _, n = scales.shape
    words = np.ascontiguousarray(words).reshape(g, 128, n, -1)
    if fmt == "e4m3":
        vals = words.view(ml_dtypes.float8_e4m3fn).astype(np.float64)
    else:
        nib = np.empty((g, 128, n, 4), np.uint8)
        nib[..., 0::2] = words & 0xF
        nib[..., 1::2] = words >> 4
        vals = E2M1[nib]
    vals = vals * np.repeat(np.exp2(scales.astype(np.float64) - 127.0), 8, axis=1)[..., None]
    return vals.transpose(0, 1, 3, 2).reshape(g * 512, n)


def gelu(v):
    return 0.5 * v * (1.0 + np.tanh(np.sqrt(2.0 / np.pi) * (v + 0.044715 * v**3)))


def often(T, S):
    return np.random.permutation(T)[(T * np.random.uniform(0, 1, S) ** 4).astype(np.int64)]


K, T, S, T2, P, H, N = 1024, 2048, 1024, 2048, 512, 1024, 512

def setup_inputs():
    n = np.random.standard_normal
    s = mx_kscale(K)[:, None]
    u = mx_kscale(H)[:, None]
    tab_words, tab_scales = pack_weight(n((K, T)) * s, "e4m3")
    tab2_words, tab2_scales = pack_weight(n((K, T2)) * s, "e4m3")
    w2_words, w2_scales = pack_weight(n((K, H)) / np.sqrt(K) / s * u.T, "e2m1")
    w4_words, w4_scales = pack_weight(n((H, N)) / np.sqrt(H) / u, "e4m3")
    return {
        "tab_words": tab_words, "tab_scales": tab_scales,
        "offs": striped(np.random.permutation(T)[:S]),
        "pos1": striped(often(S, P)),
        "tab2_words": tab2_words, "tab2_scales": tab2_scales,
        "offs2": striped(np.random.permutation(T2)[:P]),
        "w1": (n((K, H)) / np.sqrt(K) / s * u.T).astype(np.float32),
        "b1": (0.5 * n(H) * u[:, 0]).astype(np.float32),
        "w2_words": w2_words, "w2_scales": w2_scales,
        "b2": (0.5 * n(H) * u[:, 0]).astype(np.float32),
        "w3": (n((H, N)) / np.sqrt(H) / u).astype(np.float32),
        "w4_words": w4_words, "w4_scales": w4_scales,
        "d": (0.5 * n(N)).astype(np.float32),
    }

def reference(tab_words, tab_scales, offs, pos1, tab2_words, tab2_scales, offs2, w1, b1,
              w2_words, w2_scales, b2, w3, w4_words, w4_scales, d):
    v = unpack_weight(tab_words, tab_scales, "e4m3")[:, unstriped(offs)]
    v2 = unpack_weight(tab2_words, tab2_scales, "e4m3")[:, unstriped(offs2)]
    h = (mxq(f64(w1), 0, "e4m3").T @ v) + f64(b1)[:, None]
    x = h[:, unstriped(pos1)]
    e = (unpack_weight(w2_words, w2_scales, "e2m1").T @ v2) + f64(b2)[:, None]
    hi = mxq(np.maximum(x, e), 0, "e4m3")
    lo = mxq(np.minimum(x, e), 0, "e4m3")
    w4 = unpack_weight(w4_words, w4_scales, "e4m3")
    y = mxq(f64(w3), 0, "e4m3").T @ hi + w4.T @ lo
    return y + f64(d)[:, None]

@@ -1,0 +1,256 @@
+from contextlib import ExitStack
+
+import concourse.mybir as mybir
+
+K, T, S, T2, M, H, N = 1024, 2048, 1024, 2048, 512, 1024, 512
+FLOPS = 2 * K * H * S + 2 * K * H * M + 2 * 2 * H * N * M
+
+F32 = mybir.dt.float32
+BF16 = mybir.dt.bfloat16
+I32 = mybir.dt.int32
+U32 = mybir.dt.uint32
+U16 = mybir.dt.uint16
+U8 = mybir.dt.uint8
+FP8X4 = mybir.dt.float8_e4m3fn_x4
+FP4X4 = mybir.dt.float4_e2m1fn_x4
+ALU = mybir.AluOpType
+IDENT = mybir.ActivationFunctionType.Identity
+
+P = 128
+PACK = 4
+PASS = P * PACK
+BANK = 512
+
+
+def tile_list_fit_margins_kernel(tc, tab_words, tab_scales, offs, pos1, tab2_words, tab2_scales, offs2,
+                                           w1, b1, w2_words, w2_scales, b2, w3, w4_words, w4_scales, d, out):
+    nc = tc.nc
+    with ExitStack() as ctx:
+        lists = ctx.enter_context(tc.tile_pool(name="lists", bufs=1))
+        keep = ctx.enter_context(tc.tile_pool(name="keep", bufs=1))
+        psum = ctx.enter_context(tc.psum_pool(name="psum", bufs=1))
+
+        def held(name, shape, dtype, tag=None, bufs=1):
+            return keep.tile(shape, dtype, name=name, tag=tag or name, bufs=bufs, align_bytes=64)
+
+        def load_list(name, src):
+            t = lists.tile(list(src.shape), U16, name=name)
+            nc.sync.dma_start(t[:], src)
+            return t
+
+        def load_words(name, src):
+            t = held(name, [P, src.shape[1]], U32)
+            nc.sync.dma_start(t[:].bitcast(I32), src.rearrange("p c i -> p (c i)").bitcast(I32))
+            return t
+
+        def zeroed(name, width):
+            t = held(name, [P, width], U8)
+            nc.vector.memset(t[:].bitcast(I32), 0)
+            return t
+
+        def load_scales_stacked(t, src, queue):
+            for q in range(4):
+                queue.dma_start(t[32 * q:32 * q + 8, :].bitcast(I32), src[:, 4 * q:4 * q + 4, :].bitcast(I32))
+
+        def load_rows(name, rows):
+            t = held(name, [P, PACK, BANK], F32, tag="raw", bufs=4)
+            nc.sync.dma_start(t[:], rows.rearrange("(p j) c -> p j c", j=PACK))
+            return t
+
+        def copy(engine, dst, src):
+            if engine == "S":
+                nc.scalar.copy(dst, src)
+            else:
+                nc.vector.tensor_copy(dst, src)
+
+        def interleave(engine, name, planes, tag, bufs):
+            t = held(name, [P, planes.shape[2] * PACK], BF16, tag=tag, bufs=bufs)
+            copy(engine, t[:].rearrange("p (c i j) -> p c j i", i=4, j=PACK),
+                 planes.rearrange("p j (c i) -> p c j i", i=4))
+            return t
+
+        def interleave_permuted(engine, name, planes):
+            t = held(name, [P, BANK * PACK], BF16, tag="wbf", bufs=3)
+            copy(engine, t[:].rearrange("p (t m j) -> p m j t", t=PACK, j=PACK),
+                 planes[:].rearrange("p j (m t) -> p m j t", t=PACK))
+            return t
+
+        def quantize(name, grouped):
+            width = grouped.shape[1] // PACK
+            codes = held(name + "_codes", [P, width], U32)
+            scales = held(name + "_scales", [P, width], U8)
+            nc.vector.quantize_mx(out=codes[:].bitcast(FP8X4), scales=scales[:], in_=grouped[:])
+            return codes, scales
+
+        def second_plane(name, stacked, width):
+            t = zeroed(name, width)
+            return t, lambda: nc.gpsimd.dma_start(t[0:112, :].bitcast(I32), stacked[4:116, :].bitcast(I32))
+
+        tab_sc = zeroed("tab_sc", T)
+        tab2_sc = zeroed("tab2_sc", T2)
+        w2_sc_raw = zeroed("w2_sc_raw", H)
+        w4_sc = zeroed("w4_sc", N)
+        v2_sc = held("v2_sc", [P, M], U8)
+        w2_sc = held("w2_sc", [P, H], U8)
+        v2_sc1, move_v2_sc = second_plane("v2_sc1", v2_sc, M)
+        w2_sc1, move_w2_sc = second_plane("w2_sc1", w2_sc, H)
+
+        load_scales_stacked(tab_sc, tab_scales, nc.scalar)
+        offs_t = load_list("offs_t", offs)
+        b1_t = held("b1_t", [P, 2, PACK], F32)
+        nc.sync.dma_start(b1_t[:], b1.rearrange("(b p t) -> p b t", b=2, t=PACK))
+        tab_w = [load_words("tab_w0", tab_words[0])]
+        offs2_t = load_list("offs2_t", offs2)
+        w1_raw = {}
+        w1_raw[0, 0] = load_rows("w1_raw00", w1[0:PASS, 0:BANK])
+        pos_t = load_list("pos_t", pos1)
+        tab_w.append(load_words("tab_w1", tab_words[1]))
+        b2_t = held("b2_t", [P, 2, PACK], F32)
+        nc.sync.dma_start(b2_t[:], b2.rearrange("(b p t) -> p b t", b=2, t=PACK))
+        load_scales_stacked(tab2_sc, tab2_scales, nc.sync)
+        w1_raw[0, 1] = load_rows("w1_raw01", w1[PASS:K, 0:BANK])
+        d_t = held("d_t", [P, N // P], F32)
+        with nc.allow_non_contiguous_dma(reason="one bias value for each partition"):
+            nc.sync.dma_start(d_t[:], d.rearrange("(c p) -> p c", p=P))
+        w1_raw[1, 0] = load_rows("w1_raw10", w1[0:PASS, BANK:H])
+        w2_raw = held("w2_raw", [P, 2, 2 * H], U8)
+        nc.sync.dma_start(w2_raw[:].bitcast(I32), w2_words.rearrange("a p c -> p a c").bitcast(I32))
+        load_scales_stacked(w2_sc_raw, w2_scales, nc.sync)
+        w1_raw[1, 1] = load_rows("w1_raw11", w1[PASS:K, BANK:H])
+        load_scales_stacked(w4_sc, w4_scales, nc.sync)
+        tab2_w = [load_words("tab2_w%d" % a, tab2_words[a]) for a in range(2)]
+        w4_w = [load_words("w4_w%d" % b, w4_words[b]) for b in range(2)]
+        w3_raw = [load_rows("w3_raw%d" % b, w3[b * PASS:(b + 1) * PASS, :]) for b in range(2)]
+
+        w1_q = {}
+
+        def bank(name, width):
+            return psum.tile([P, width], F32, name=name, tag="bank", bufs=8)
+
+        def cast_w1(engine, b, a):
+            return interleave_permuted(engine, "w1_bf%d%d" % (b, a), w1_raw[b, a])
+
+        def gather_words(name, window, offsets, pieces):
+            n = offsets.shape[1] * 16
+            t = held(name, [P, n], U32)
+            step = n // pieces
+            for i in range(pieces):
+                nc.vector.tensor_copy(t[:, i * step:(i + 1) * step],
+                                      window[:].indirect(offsets[:, i * step // 16:(i + 1) * step // 16]))
+            return t
+
+        h = {}
+
+        def project_assemblies(b):
+            for t in range(PACK):
+                h[b, t] = held("h%d%d" % (b, t), [P, S], F32)
+                rows = slice(t * P, (t + 1) * P)
+                for half in range(S // BANK):
+                    cols = slice(half * BANK, (half + 1) * BANK)
+                    acc = bank("acc", BANK)
+                    for a in range(2):
+                        codes, scales = w1_q[b, a]
+                        nc.tensor.matmul_mx(out=acc[:], lhsT=codes[:, rows].bitcast(FP8X4), lhsT_scale=scales[:, rows],
+                                            rhs=v_w[a][:, cols].bitcast(FP8X4), rhs_scale=v_sc[4 * a:P, cols],
+                                            start=(a == 0), stop=(a == 1))
+                    nc.scalar.activation(h[b, t][:, cols], acc[:], IDENT, bias=b1_t[:, b, t:t + 1])
+
+        def project_components(b):
+            e = held("e%d" % b, [P, PACK, M], F32, tag="e", bufs=2)
+            for t in range(PACK):
+                acc = bank("acc", BANK)
+                c0 = b * BANK + t * P
+                for a in range(2):
+                    nc.tensor.matmul_mx(out=acc[:], lhsT=w2_w[:, a, 2 * c0:2 * (c0 + P)].bitcast(FP4X4),
+                                        lhsT_scale=(w2_sc, w2_sc1)[a][:, c0:c0 + P],
+                                        rhs=v2_w[a][:].bitcast(FP8X4), rhs_scale=(v2_sc, v2_sc1)[a][:],
+                                        start=(a == 0), stop=(a == 1))
+                nc.scalar.activation(e[:, t, :], acc[:], IDENT, bias=b2_t[:, b, t:t + 1])
+            return interleave("S", "e_bf%d" % b, e[:], "e_bf", 2)
+
+        def fetch(engine, b, m0, width):
+            x = held("x%d_%d" % (b, m0), [P, PACK, width], F32, tag="x", bufs=1)
+            for t in range(PACK):
+                nc.vector.tensor_copy(x[:, t, :], h[b, t][:].indirect(pos_t[:, m0 // 16:(m0 + width) // 16]))
+            return interleave(engine, "x_bf%d_%d" % (b, m0), x[:], "x_bf", 2)
+
+        def order(b, m0, width, x_bf, e_bf):
+            name = "%d_%d" % (b, m0)
+            hi = held("hi" + name, [P, width * PACK], BF16, tag="hi")
+            lo = held("lo" + name, [P, width * PACK], BF16, tag="lo")
+            e_part = e_bf[:, m0 * PACK:(m0 + width) * PACK]
+            nc.vector.tensor_tensor(hi[:], x_bf[:], e_part, ALU.max)
+            nc.vector.tensor_tensor(lo[:], x_bf[:], e_part, ALU.min)
+            return quantize("hi_q" + name, hi), quantize("lo_q" + name, lo)
+
+        HALF = M // 2
+        y = {}
+
+        def score(b, side, half, operand, m0, start, stop):
+            codes, scales = operand
+            mc = slice(half * HALF - m0, (half + 1) * HALF - m0)
+            for c in range(N // P):
+                if start:
+                    y[c, half] = bank("y", HALF)
+                cols = slice(c * P, (c + 1) * P)
+                if side == 0:
+                    w, ws = w3_q[b][0][:, cols], w3_q[b][1][:, cols]
+                else:
+                    w, ws = w4_w[b][:, cols], w4_sc[4 * b:P, cols]
+                nc.tensor.matmul_mx(out=y[c, half][:], lhsT=w.bitcast(FP8X4), lhsT_scale=ws,
+                                    rhs=codes[:, mc].bitcast(FP8X4), rhs_scale=scales[:, mc], start=start, stop=stop)
+
+        def store(half, engines):
+            for c in range(N // P):
+                res = held("res%d%d" % (c, half), [P, HALF], F32)
+                if engines[c] == "S":
+                    nc.scalar.activation(res[:], y[c, half][:], IDENT, bias=d_t[:, c:c + 1])
+                else:
+                    nc.vector.tensor_scalar(res[:], y[c, half][:], d_t[:, c:c + 1], None, ALU.add)
+                nc.sync.dma_start(out[c * P:(c + 1) * P, half * HALF:(half + 1) * HALF], res[:])
+
+        v_sc = held("v_sc", [P, S], U8)
+        nc.vector.tensor_copy(v_sc[:], tab_sc[:].indirect(offs_t[:]))
+        bf = cast_w1("S", 0, 0)
+        v_w = [gather_words("v_w0", tab_w[0], offs_t, 1)]
+        w1_q[0, 0] = quantize("w1_q00", bf)
+        bf = cast_w1("S", 0, 1)
+        v_w.append(gather_words("v_w1", tab_w[1], offs_t, 2))
+        w1_q[0, 1] = quantize("w1_q01", bf)
+        project_assemblies(0)
+        w1_q[1, 0] = quantize("w1_q10", cast_w1("S", 1, 0))
+        w1_q[1, 1] = quantize("w1_q11", cast_w1("V", 1, 1))
+        project_assemblies(1)
+
+        nc.vector.tensor_copy(v2_sc[:], tab2_sc[:].indirect(offs2_t[:]))
+        move_v2_sc()
+        w2_w = held("w2_w", [P, 2, 2 * H], U8)
+        nc.vector.tensor_copy(
+            w2_w[:].rearrange("p a c -> p (a c)").bitcast(U16).rearrange("p (g t m) -> p g t m", t=PACK, m=P),
+            w2_raw[:].rearrange("p a c -> p (a c)").bitcast(U16).rearrange("p (g m t) -> p g t m", t=PACK, m=P))
+        nc.vector.tensor_copy(w2_sc[:].rearrange("p (g t m) -> p g t m", t=PACK, m=P),
+                              w2_sc_raw[:].rearrange("p (g m t) -> p g t m", t=PACK, m=P))
+        move_w2_sc()
+        v2_w = [gather_words("v2_w%d" % a, tab2_w[a], offs2_t, 1) for a in range(2)]
+
+        x0 = fetch("V", 0, 0, M)
+        e0 = project_components(0)
+        hi0, lo0 = order(0, 0, M, x0, e0)
+        e1 = project_components(1)
+        w3_q = []
+        for b in range(2):
+            w3_q.append(quantize("w3_q%d" % b, interleave("S", "w3_bf%d" % b, w3_raw[b][:], "wbf", 3)))
+        for half in range(2):
+            score(0, 1, half, lo0, 0, True, False)
+        for half in range(2):
+            score(0, 0, half, hi0, 0, False, False)
+        x1 = fetch("V", 1, 0, HALF)
+        hi1, lo1 = order(1, 0, HALF, x1, e1)
+        x1 = fetch("V", 1, HALF, HALF)
+        score(1, 0, 0, hi1, 0, False, False)
+        score(1, 1, 0, lo1, 0, False, True)
+        store(0, "SSSS")
+        hi1, lo1 = order(1, HALF, HALF, x1, e1)
+        score(1, 0, 1, hi1, HALF, False, False)
+        score(1, 1, 1, lo1, HALF, False, True)
+        store(1, "SVSV")

@@ -1,6 +1,7 @@
 from contextlib import ExitStack
 
 import concourse.mybir as mybir
+from concourse.masks import make_identity
 
 K, T, S, T2, M, H, N = 1024, 2048, 1024, 2048, 512, 1024, 512
 FLOPS = 2 * K * H * S + 2 * K * H * M + 2 * 2 * H * N * M
@@ -20,6 +21,7 @@ P = 128
 PACK = 4
 PASS = P * PACK
 BANK = 512
+SHARED = {"tab2_w0":"slotA","x0_0":"slotA","w1_bf11":"slotB","x0_256":"slotB","w1_raw11":"slotC","eT0":"slotC"}
 
 
 def tile_list_fit_margins_kernel(tc, tab_words, tab_scales, offs, pos1, tab2_words, tab2_scales, offs2,
@@ -31,6 +33,8 @@ def tile_list_fit_margins_kernel(tc, tab_words, tab_scales, offs, pos1, tab2_wor
         psum = ctx.enter_context(tc.psum_pool(name="psum", bufs=1))
 
         def held(name, shape, dtype, tag=None, bufs=1):
+            if name in SHARED:
+                tag, bufs = SHARED[name], 1
             return keep.tile(shape, dtype, name=name, tag=tag or name, bufs=bufs, align_bytes=64)
 
         def load_list(name, src):
@@ -53,13 +57,15 @@ def tile_list_fit_margins_kernel(tc, tab_words, tab_scales, offs, pos1, tab2_wor
                 queue.dma_start(t[32 * q:32 * q + 8, :].bitcast(I32), src[:, 4 * q:4 * q + 4, :].bitcast(I32))
 
         def load_rows(name, rows):
-            t = held(name, [P, PACK, BANK], F32, tag="raw", bufs=4)
+            t = held(name, [P, PACK, BANK], F32, tag="raw", bufs=3)
             nc.sync.dma_start(t[:], rows.rearrange("(p j) c -> p j c", j=PACK))
             return t
 
         def copy(engine, dst, src):
             if engine == "S":
                 nc.scalar.copy(dst, src)
+            elif engine == "G":
+                nc.gpsimd.tensor_scalar(dst, src, 1.0, 0.0, ALU.mult, ALU.add)
             else:
                 nc.vector.tensor_copy(dst, src)
 
@@ -82,50 +88,49 @@ def tile_list_fit_margins_kernel(tc, tab_words, tab_scales, offs, pos1, tab2_wor
             nc.vector.quantize_mx(out=codes[:].bitcast(FP8X4), scales=scales[:], in_=grouped[:])
             return codes, scales
 
-        def second_plane(name, stacked, width):
-            t = zeroed(name, width)
-            return t, lambda: nc.gpsimd.dma_start(t[0:112, :].bitcast(I32), stacked[4:116, :].bitcast(I32))
+        def load_scales_side_by_side(t, src):
+            for q in range(4):
+                nc.sync.dma_start(t[32 * q:32 * q + 4, :].bitcast(I32).rearrange("r (a c) -> r a c", a=2),
+                                  src[:, 4 * q:4 * q + 4, :].bitcast(I32).rearrange("a r c -> r a c"))
 
         tab_sc = zeroed("tab_sc", T)
-        tab2_sc = zeroed("tab2_sc", T2)
-        w2_sc_raw = zeroed("w2_sc_raw", H)
-        w4_sc = zeroed("w4_sc", N)
-        v2_sc = held("v2_sc", [P, M], U8)
-        w2_sc = held("w2_sc", [P, H], U8)
-        v2_sc1, move_v2_sc = second_plane("v2_sc1", v2_sc, M)
-        w2_sc1, move_w2_sc = second_plane("w2_sc1", w2_sc, H)
-
-        load_scales_stacked(tab_sc, tab_scales, nc.scalar)
-        offs_t = load_list("offs_t", offs)
+        tab2_sc = zeroed("tab2_sc", 2 * T2)
+        w2_sc_raw = zeroed("w2_sc_raw", 2 * H)
+        w4_sc = zeroed("w4_sc", 2 * N)
         b1_t = held("b1_t", [P, 2, PACK], F32)
-        nc.sync.dma_start(b1_t[:], b1.rearrange("(b p t) -> p b t", b=2, t=PACK))
-        tab_w = [load_words("tab_w0", tab_words[0])]
+        b2_t = held("b2_t", [P, 2, PACK], F32)
+        d_t = held("d_t", [P, N // P], F32)
+        w2_raw = held("w2_raw", [P, 2, 2 * H], U8)
+        w4_w = held("w4_w", [P, 2, N], U32)
+        tab_w, tab2_w, w1_raw, w3_raw = {}, {}, {}, {}
+        load_scales_stacked(tab_sc, tab_scales, nc.sync)
+        offs_t = load_list("offs_t", offs)
+        nc.sync.dma_start(b2_t[:], b2.rearrange("(b p t) -> p b t", b=2, t=PACK))
         offs2_t = load_list("offs2_t", offs2)
-        w1_raw = {}
+        tab_w[0] = load_words("tab_w0", tab_words[0])
         w1_raw[0, 0] = load_rows("w1_raw00", w1[0:PASS, 0:BANK])
         pos_t = load_list("pos_t", pos1)
-        tab_w.append(load_words("tab_w1", tab_words[1]))
-        b2_t = held("b2_t", [P, 2, PACK], F32)
-        nc.sync.dma_start(b2_t[:], b2.rearrange("(b p t) -> p b t", b=2, t=PACK))
-        load_scales_stacked(tab2_sc, tab2_scales, nc.sync)
+        tab_w[1] = load_words("tab_w1", tab_words[1])
+        nc.sync.dma_start(b1_t[:], b1.rearrange("(b p t) -> p b t", b=2, t=PACK))
         w1_raw[0, 1] = load_rows("w1_raw01", w1[PASS:K, 0:BANK])
-        d_t = held("d_t", [P, N // P], F32)
+        w1_raw[1, 0] = load_rows("w1_raw10", w1[0:PASS, BANK:H])
+        load_scales_side_by_side(tab2_sc, tab2_scales)
+        tab2_w[0] = load_words("tab2_w0", tab2_words[0])
         with nc.allow_non_contiguous_dma(reason="one bias value for each partition"):
             nc.sync.dma_start(d_t[:], d.rearrange("(c p) -> p c", p=P))
-        w1_raw[1, 0] = load_rows("w1_raw10", w1[0:PASS, BANK:H])
-        w2_raw = held("w2_raw", [P, 2, 2 * H], U8)
+        tab2_w[1] = load_words("tab2_w1", tab2_words[1])
         nc.sync.dma_start(w2_raw[:].bitcast(I32), w2_words.rearrange("a p c -> p a c").bitcast(I32))
-        load_scales_stacked(w2_sc_raw, w2_scales, nc.sync)
+        load_scales_side_by_side(w2_sc_raw, w2_scales)
         w1_raw[1, 1] = load_rows("w1_raw11", w1[PASS:K, BANK:H])
-        load_scales_stacked(w4_sc, w4_scales, nc.sync)
-        tab2_w = [load_words("tab2_w%d" % a, tab2_words[a]) for a in range(2)]
-        w4_w = [load_words("w4_w%d" % b, w4_words[b]) for b in range(2)]
-        w3_raw = [load_rows("w3_raw%d" % b, w3[b * PASS:(b + 1) * PASS, :]) for b in range(2)]
+        load_scales_side_by_side(w4_sc, w4_scales)
+        w3_raw[0] = load_rows("w3_raw0", w3[0:PASS, :])
+        w3_raw[1] = load_rows("w3_raw1", w3[PASS:H, :])
+        nc.sync.dma_start(w4_w[:].bitcast(I32), w4_words.rearrange("a p c i -> p a (c i)").bitcast(I32))
 
         w1_q = {}
 
-        def bank(name, width):
-            return psum.tile([P, width], F32, name=name, tag="bank", bufs=8)
+        def bank(name, width, index):
+            return psum.tile([P, width], F32, name=name, tag="bank%d" % index)
 
         def cast_w1(engine, b, a):
             return interleave_permuted(engine, "w1_bf%d%d" % (b, a), w1_raw[b, a])
@@ -147,7 +152,7 @@ def tile_list_fit_margins_kernel(tc, tab_words, tab_scales, offs, pos1, tab2_wor
                 rows = slice(t * P, (t + 1) * P)
                 for half in range(S // BANK):
                     cols = slice(half * BANK, (half + 1) * BANK)
-                    acc = bank("acc", BANK)
+                    acc = bank("acc", BANK, 2 * t + half)
                     for a in range(2):
                         codes, scales = w1_q[b, a]
                         nc.tensor.matmul_mx(out=acc[:], lhsT=codes[:, rows].bitcast(FP8X4), lhsT_scale=scales[:, rows],
@@ -155,24 +160,45 @@ def tile_list_fit_margins_kernel(tc, tab_words, tab_scales, offs, pos1, tab2_wor
                                             start=(a == 0), stop=(a == 1))
                     nc.scalar.activation(h[b, t][:, cols], acc[:], IDENT, bias=b1_t[:, b, t:t + 1])
 
-        def project_components(b):
-            e = held("e%d" % b, [P, PACK, M], F32, tag="e", bufs=2)
-            for t in range(PACK):
-                acc = bank("acc", BANK)
-                c0 = b * BANK + t * P
-                for a in range(2):
-                    nc.tensor.matmul_mx(out=acc[:], lhsT=w2_w[:, a, 2 * c0:2 * (c0 + P)].bitcast(FP4X4),
-                                        lhsT_scale=(w2_sc, w2_sc1)[a][:, c0:c0 + P],
-                                        rhs=v2_w[a][:].bitcast(FP8X4), rhs_scale=(v2_sc, v2_sc1)[a][:],
-                                        start=(a == 0), stop=(a == 1))
-                nc.scalar.activation(e[:, t, :], acc[:], IDENT, bias=b2_t[:, b, t:t + 1])
-            return interleave("S", "e_bf%d" % b, e[:], "e_bf", 2)
+        ident = held("ident", [P, P], F32)
+        make_identity(nc, ident[:])
+        b2_row = held("b2_row", [P, 2, PACK, P], F32)
 
-        def fetch(engine, b, m0, width):
-            x = held("x%d_%d" % (b, m0), [P, PACK, width], F32, tag="x", bufs=1)
+        def spread_bias():
+            for b in range(2):
+                acc = bank("spread", BANK, 6 + b)
+                for t in range(PACK):
+                    nc.tensor.transpose(acc[:, t * P:(t + 1) * P], b2_t[:, b, t:t + 1].to_broadcast([P, P]), ident[:])
+                nc.scalar.copy(b2_row[:, b, :, :].rearrange("p t m -> p (t m)"), acc[:])
+
+        def project_components(b):
+            e_t = held("eT%d" % b, [P, M // P, PACK, P], F32, tag="eT", bufs=2)
+            e_bf = held("e_bf%d" % b, [P, M * PACK], BF16)
+            for c in range(M // P):
+                acc = bank("acc", BANK, c)
+                cols = slice(c * P, (c + 1) * P)
+                for a in range(2):
+                    nc.tensor.matmul_mx(out=acc[:], lhsT=v2_w[a][:, cols].bitcast(FP8X4), lhsT_scale=v2_sc[:, a, cols],
+                                        rhs=w2_raw[:, a, 2 * b * BANK:2 * (b + 1) * BANK].bitcast(FP4X4),
+                                        rhs_scale=w2_sc_raw[:, a * H + b * BANK:a * H + (b + 1) * BANK],
+                                        start=(a == 0), stop=(a == 1))
+                nc.scalar.copy(e_t[:, c, :, :], acc[:].rearrange("m (p t) -> m t p", t=PACK))
+                turned = bank("turned", BANK, 4 + c)
+                for t in range(PACK):
+                    nc.tensor.matmul(turned[:, t * P:(t + 1) * P], lhsT=b2_row[:, b, t, :], rhs=ident[:], is_transpose=True,
+                                     start=(t == 0), stop=False)
+                for t in range(PACK):
+                    nc.tensor.matmul(turned[:, t * P:(t + 1) * P], lhsT=e_t[:, c, t, :], rhs=ident[:], is_transpose=True,
+                                     start=False, stop=(t == PACK - 1))
+                nc.scalar.copy(e_bf[:, c * P * PACK:(c + 1) * P * PACK].rearrange("p (m t) -> p m t", t=PACK),
+                               turned[:].rearrange("p (t m) -> p m t", t=PACK))
+            return e_bf
+
+        def fetch(engine, b, m0, width, dst):
+            x = held("x%d_%d" % (b, m0), [P, PACK, width], F32, tag="x")
             for t in range(PACK):
                 nc.vector.tensor_copy(x[:, t, :], h[b, t][:].indirect(pos_t[:, m0 // 16:(m0 + width) // 16]))
-            return interleave(engine, "x_bf%d_%d" % (b, m0), x[:], "x_bf", 2)
+            copy(engine, dst.rearrange("p (c i j) -> p c j i", i=4, j=PACK), x[:].rearrange("p j (c i) -> p c j i", i=4))
 
         def order(b, m0, width, x_bf, e_bf):
             name = "%d_%d" % (b, m0)
@@ -191,12 +217,12 @@ def tile_list_fit_margins_kernel(tc, tab_words, tab_scales, offs, pos1, tab2_wor
             mc = slice(half * HALF - m0, (half + 1) * HALF - m0)
             for c in range(N // P):
                 if start:
-                    y[c, half] = bank("y", HALF)
+                    y[c, half] = bank("y", HALF, c + 4 * half)
                 cols = slice(c * P, (c + 1) * P)
                 if side == 0:
                     w, ws = w3_q[b][0][:, cols], w3_q[b][1][:, cols]
                 else:
-                    w, ws = w4_w[b][:, cols], w4_sc[4 * b:P, cols]
+                    w, ws = w4_w[:, b, cols], w4_sc[:, b * N + c * P:b * N + (c + 1) * P]
                 nc.tensor.matmul_mx(out=y[c, half][:], lhsT=w.bitcast(FP8X4), lhsT_scale=ws,
                                     rhs=codes[:, mc].bitcast(FP8X4), rhs_scale=scales[:, mc], start=start, stop=stop)
 
@@ -209,48 +235,50 @@ def tile_list_fit_margins_kernel(tc, tab_words, tab_scales, offs, pos1, tab2_wor
                     nc.vector.tensor_scalar(res[:], y[c, half][:], d_t[:, c:c + 1], None, ALU.add)
                 nc.sync.dma_start(out[c * P:(c + 1) * P, half * HALF:(half + 1) * HALF], res[:])
 
+        v_w, v2_w, w3_q = {}, {}, {}
+        spread_bias()
         v_sc = held("v_sc", [P, S], U8)
         nc.vector.tensor_copy(v_sc[:], tab_sc[:].indirect(offs_t[:]))
-        bf = cast_w1("S", 0, 0)
-        v_w = [gather_words("v_w0", tab_w[0], offs_t, 1)]
-        w1_q[0, 0] = quantize("w1_q00", bf)
-        bf = cast_w1("S", 0, 1)
-        v_w.append(gather_words("v_w1", tab_w[1], offs_t, 2))
-        w1_q[0, 1] = quantize("w1_q01", bf)
+        v_w[0] = gather_words("v_w0", tab_w[0], offs_t, 1)
+        bf00 = cast_w1("S", 0, 0)
+        v_w[1] = gather_words("v_w1", tab_w[1], offs_t, 2)
+        w1_q[0, 0] = quantize("w1_q00", bf00)
+        bf01 = cast_w1("S", 0, 1)
+        w1_q[0, 1] = quantize("w1_q01", bf01)
+        v2_sc = held("v2_sc", [P, 2, M], U8)
+        for a in range(2):
+            nc.vector.tensor_copy(v2_sc[:, a, :], tab2_sc[:, a * T2:(a + 1) * T2].indirect(offs2_t[:]))
+        bf10 = cast_w1("S", 1, 0)
         project_assemblies(0)
-        w1_q[1, 0] = quantize("w1_q10", cast_w1("S", 1, 0))
-        w1_q[1, 1] = quantize("w1_q11", cast_w1("V", 1, 1))
-        project_assemblies(1)
-
-        nc.vector.tensor_copy(v2_sc[:], tab2_sc[:].indirect(offs2_t[:]))
-        move_v2_sc()
-        w2_w = held("w2_w", [P, 2, 2 * H], U8)
-        nc.vector.tensor_copy(
-            w2_w[:].rearrange("p a c -> p (a c)").bitcast(U16).rearrange("p (g t m) -> p g t m", t=PACK, m=P),
-            w2_raw[:].rearrange("p a c -> p (a c)").bitcast(U16).rearrange("p (g m t) -> p g t m", t=PACK, m=P))
-        nc.vector.tensor_copy(w2_sc[:].rearrange("p (g t m) -> p g t m", t=PACK, m=P),
-                              w2_sc_raw[:].rearrange("p (g m t) -> p g t m", t=PACK, m=P))
-        move_w2_sc()
-        v2_w = [gather_words("v2_w%d" % a, tab2_w[a], offs2_t, 1) for a in range(2)]
-
-        x0 = fetch("V", 0, 0, M)
+        w1_q[1, 0] = quantize("w1_q10", bf10)
+        v2_w[0] = gather_words("v2_w0", tab2_w[0], offs2_t, 1)
+        v2_w[1] = gather_words("v2_w1", tab2_w[1], offs2_t, 1)
+        bf11 = cast_w1("S", 1, 1)
+        x0 = held("x_bf0", [P, M * PACK], BF16, tag="x_bf")
+        fetch("V", 0, 0, HALF, x0[:, 0:HALF * PACK])
+        w1_q[1, 1] = quantize("w1_q11", bf11)
+        fetch("V", 0, HALF, HALF, x0[:, HALF * PACK:M * PACK])
         e0 = project_components(0)
+        project_assemblies(1)
+        bf30 = interleave("V", "w3_bf0", w3_raw[0][:], "wbf", 3)
+        w3_q[0] = quantize("w3_q0", bf30)
         hi0, lo0 = order(0, 0, M, x0, e0)
         e1 = project_components(1)
-        w3_q = []
-        for b in range(2):
-            w3_q.append(quantize("w3_q%d" % b, interleave("S", "w3_bf%d" % b, w3_raw[b][:], "wbf", 3)))
-        for half in range(2):
-            score(0, 1, half, lo0, 0, True, False)
-        for half in range(2):
-            score(0, 0, half, hi0, 0, False, False)
-        x1 = fetch("V", 1, 0, HALF)
-        hi1, lo1 = order(1, 0, HALF, x1, e1)
-        x1 = fetch("V", 1, HALF, HALF)
-        score(1, 0, 0, hi1, 0, False, False)
-        score(1, 1, 0, lo1, 0, False, True)
+        bf31 = interleave("S", "w3_bf1", w3_raw[1][:], "wbf", 3)
+        w3_q[1] = quantize("w3_q1", bf31)
+        score(0, 1, 0, lo0, 0, True, False)
+        score(0, 0, 0, hi0, 0, False, False)
+        x10 = held("x_bf10", [P, HALF * PACK], BF16, tag="x_bf")
+        fetch("V", 1, 0, HALF, x10[:])
+        hi10, lo10 = order(1, 0, HALF, x10, e1)
+        x11 = held("x_bf11", [P, HALF * PACK], BF16, tag="x_bf")
+        fetch("V", 1, HALF, HALF, x11[:])
+        score(0, 1, 1, lo0, 0, True, False)
+        score(0, 0, 1, hi0, 0, False, False)
+        score(1, 0, 0, hi10, 0, False, False)
+        score(1, 1, 0, lo10, 0, False, True)
         store(0, "SSSS")
-        hi1, lo1 = order(1, HALF, HALF, x1, e1)
-        score(1, 0, 1, hi1, HALF, False, False)
-        score(1, 1, 1, lo1, HALF, False, True)
+        hi11, lo11 = order(1, HALF, HALF, x11, e1)
+        score(1, 0, 1, hi11, HALF, False, False)
+        score(1, 1, 1, lo11, HALF, False, True)
         store(1, "SVSV")

@@ -15,13 +15,15 @@ U8 = mybir.dt.uint8
 FP8X4 = mybir.dt.float8_e4m3fn_x4
 FP4X4 = mybir.dt.float4_e2m1fn_x4
 ALU = mybir.AluOpType
-IDENT = mybir.ActivationFunctionType.Identity
+IDENTITY = mybir.ActivationFunctionType.Identity
 
 P = 128
 PACK = 4
 PASS = P * PACK
 BANK = 512
-SHARED = {"tab2_w0":"slotA","x0_0":"slotA","w1_bf11":"slotB","x0_256":"slotB","w1_raw11":"slotC","eT0":"slotC"}
+QUADRANTS = 4
+RUN = 4
+HALF = M // 2
 
 
 def tile_list_fit_margins_kernel(tc, tab_words, tab_scales, offs, pos1, tab2_words, tab2_scales, offs2,
@@ -29,256 +31,231 @@ def tile_list_fit_margins_kernel(tc, tab_words, tab_scales, offs, pos1, tab2_wor
     nc = tc.nc
     with ExitStack() as ctx:
         lists = ctx.enter_context(tc.tile_pool(name="lists", bufs=1))
-        keep = ctx.enter_context(tc.tile_pool(name="keep", bufs=1))
+        sbuf = ctx.enter_context(tc.tile_pool(name="sbuf", bufs=1))
         psum = ctx.enter_context(tc.psum_pool(name="psum", bufs=1))
 
-        def held(name, shape, dtype, tag=None, bufs=1):
-            if name in SHARED:
-                tag, bufs = SHARED[name], 1
-            return keep.tile(shape, dtype, name=name, tag=tag or name, bufs=bufs, align_bytes=64)
+        def tile(name, shape, dtype, tag=None, bufs=1):
+            return sbuf.tile(shape, dtype, name=name, tag=tag or name, bufs=bufs, align_bytes=64)
+
+        def bank(name, width, index):
+            return psum.tile([P, width], F32, name=name, tag="bank%d" % index)
 
         def load_list(name, src):
             t = lists.tile(list(src.shape), U16, name=name)
             nc.sync.dma_start(t[:], src)
             return t
 
-        def load_words(name, src):
-            t = held(name, [P, src.shape[1]], U32)
-            nc.sync.dma_start(t[:].bitcast(I32), src.rearrange("p c i -> p (c i)").bitcast(I32))
+        def load_table_words(name, src):
+            t = tile(name, [P, src.shape[1]], U32)
+            nc.sync.dma_start(t[:].bitcast(I32), src.rearrange("p c j -> p (c j)").bitcast(I32))
             return t
 
-        def zeroed(name, width):
-            t = held(name, [P, width], U8)
+        def zeroed_plane(name, width):
+            t = tile(name, [P, width], U8)
             nc.vector.memset(t[:].bitcast(I32), 0)
             return t
 
-        def load_scales_stacked(t, src, queue):
-            for q in range(4):
-                queue.dma_start(t[32 * q:32 * q + 8, :].bitcast(I32), src[:, 4 * q:4 * q + 4, :].bitcast(I32))
+        def load_scales_stacked(plane, src):
+            for q in range(QUADRANTS):
+                nc.sync.dma_start(plane[32 * q:32 * q + 8, :].bitcast(I32), src[:, 4 * q:4 * q + 4, :].bitcast(I32))
 
-        def load_rows(name, rows):
-            t = held(name, [P, PACK, BANK], F32, tag="raw", bufs=3)
+        def load_scales_side_by_side(plane, src):
+            for q in range(QUADRANTS):
+                nc.sync.dma_start(plane[32 * q:32 * q + 4, :].bitcast(I32).rearrange("i (a c) -> i a c", a=2),
+                                  src[:, 4 * q:4 * q + 4, :].bitcast(I32).rearrange("a i c -> i a c"))
+
+        def load_weight_pass(name, rows, tag="weight_f32", bufs=2):
+            t = tile(name, [P, PACK, BANK], F32, tag=tag, bufs=bufs)
             nc.sync.dma_start(t[:], rows.rearrange("(p j) c -> p j c", j=PACK))
             return t
 
+        def load_row_bias(name, src):
+            t = tile(name, [P, 2, PACK], F32)
+            nc.sync.dma_start(t[:], src.rearrange("(b p t) -> p b t", b=2, t=PACK))
+            return t
+
+        tab_plane = zeroed_plane("tab_plane", T)
+        tab2_plane = zeroed_plane("tab2_plane", 2 * T2)
+        w2_plane = zeroed_plane("w2_plane", 2 * H)
+        w4_plane = zeroed_plane("w4_plane", 2 * N)
+
+        tab_codes, tab2_codes, w1_f32, w3_f32 = {}, {}, {}, {}
+        load_scales_stacked(tab_plane, tab_scales)
+        offs_list = load_list("offs_list", offs)
+        b2_col = load_row_bias("b2_col", b2)
+        offs2_list = load_list("offs2_list", offs2)
+        tab_codes[0] = load_table_words("tab_codes0", tab_words[0])
+        w1_f32[0, 0] = load_weight_pass("w1_f32_00", w1[0:PASS, 0:BANK])
+        pos1_list = load_list("pos1_list", pos1)
+        tab_codes[1] = load_table_words("tab_codes1", tab_words[1])
+        b1_col = load_row_bias("b1_col", b1)
+        w1_f32[0, 1] = load_weight_pass("w1_f32_01", w1[PASS:K, 0:BANK])
+        load_scales_side_by_side(tab2_plane, tab2_scales)
+        w1_f32[1, 0] = load_weight_pass("w1_f32_10", w1[0:PASS, BANK:H], "w1_f32_10", 1)
+        d_col = tile("d_col", [P, N // P], F32)
+        with nc.allow_non_contiguous_dma(reason="one bias value for each partition"):
+            nc.sync.dma_start(d_col[:], d.rearrange("(c p) -> p c", p=P))
+        tab2_codes[0] = load_table_words("tab2_codes0", tab2_words[0])
+        tab2_codes[1] = load_table_words("tab2_codes1", tab2_words[1])
+        w2_codes = tile("w2_codes", [P, 2, 2 * H], U8)
+        nc.sync.dma_start(w2_codes[:].bitcast(I32), w2_words.rearrange("a p c -> p a c").bitcast(I32))
+        load_scales_side_by_side(w2_plane, w2_scales)
+        w1_f32[1, 1] = load_weight_pass("w1_f32_11", w1[PASS:K, BANK:H], "w1_f32_11", 1)
+        w3_f32[0] = load_weight_pass("w3_f32_0", w3[0:PASS, :])
+        load_scales_side_by_side(w4_plane, w4_scales)
+        w3_f32[1] = load_weight_pass("w3_f32_1", w3[PASS:H, :])
+        w4_codes = tile("w4_codes", [P, 2, N], U32)
+        nc.sync.dma_start(w4_codes[:].bitcast(I32), w4_words.rearrange("a p c j -> p a (c j)").bitcast(I32))
+
         def copy(engine, dst, src):
-            if engine == "S":
+            if engine is nc.scalar:
                 nc.scalar.copy(dst, src)
-            elif engine == "G":
-                nc.gpsimd.tensor_scalar(dst, src, 1.0, 0.0, ALU.mult, ALU.add)
             else:
                 nc.vector.tensor_copy(dst, src)
 
         def interleave(engine, name, planes, tag, bufs):
-            t = held(name, [P, planes.shape[2] * PACK], BF16, tag=tag, bufs=bufs)
-            copy(engine, t[:].rearrange("p (c i j) -> p c j i", i=4, j=PACK),
-                 planes.rearrange("p j (c i) -> p c j i", i=4))
+            t = tile(name, [P, planes.shape[2] * PACK], BF16, tag=tag, bufs=bufs)
+            copy(engine, t[:].rearrange("p (c i j) -> p c j i", i=RUN, j=PACK),
+                 planes.rearrange("p j (c i) -> p c j i", i=RUN))
             return t
 
-        def interleave_permuted(engine, name, planes):
-            t = held(name, [P, BANK * PACK], BF16, tag="wbf", bufs=3)
-            copy(engine, t[:].rearrange("p (t m j) -> p m j t", t=PACK, j=PACK),
-                 planes[:].rearrange("p j (m t) -> p m j t", t=PACK))
+        def interleave_w1(b, a, tag="weight_bf16", bufs=3):
+            t = tile("w1_bf16_%d%d" % (b, a), [P, BANK * PACK], BF16, tag=tag, bufs=bufs)
+            nc.scalar.copy(t[:].rearrange("p (t m j) -> p m j t", t=PACK, j=PACK),
+                           w1_f32[b, a][:].rearrange("p j (m t) -> p m j t", t=PACK))
             return t
 
         def quantize(name, grouped):
             width = grouped.shape[1] // PACK
-            codes = held(name + "_codes", [P, width], U32)
-            scales = held(name + "_scales", [P, width], U8)
+            codes = tile(name + "_codes", [P, width], U32)
+            scales = tile(name + "_scales", [P, width], U8)
             nc.vector.quantize_mx(out=codes[:].bitcast(FP8X4), scales=scales[:], in_=grouped[:])
             return codes, scales
 
-        def load_scales_side_by_side(t, src):
-            for q in range(4):
-                nc.sync.dma_start(t[32 * q:32 * q + 4, :].bitcast(I32).rearrange("r (a c) -> r a c", a=2),
-                                  src[:, 4 * q:4 * q + 4, :].bitcast(I32).rearrange("a r c -> r a c"))
-
-        tab_sc = zeroed("tab_sc", T)
-        tab2_sc = zeroed("tab2_sc", 2 * T2)
-        w2_sc_raw = zeroed("w2_sc_raw", 2 * H)
-        w4_sc = zeroed("w4_sc", 2 * N)
-        b1_t = held("b1_t", [P, 2, PACK], F32)
-        b2_t = held("b2_t", [P, 2, PACK], F32)
-        d_t = held("d_t", [P, N // P], F32)
-        w2_raw = held("w2_raw", [P, 2, 2 * H], U8)
-        w4_w = held("w4_w", [P, 2, N], U32)
-        tab_w, tab2_w, w1_raw, w3_raw = {}, {}, {}, {}
-        load_scales_stacked(tab_sc, tab_scales, nc.sync)
-        offs_t = load_list("offs_t", offs)
-        nc.sync.dma_start(b2_t[:], b2.rearrange("(b p t) -> p b t", b=2, t=PACK))
-        offs2_t = load_list("offs2_t", offs2)
-        tab_w[0] = load_words("tab_w0", tab_words[0])
-        w1_raw[0, 0] = load_rows("w1_raw00", w1[0:PASS, 0:BANK])
-        pos_t = load_list("pos_t", pos1)
-        tab_w[1] = load_words("tab_w1", tab_words[1])
-        nc.sync.dma_start(b1_t[:], b1.rearrange("(b p t) -> p b t", b=2, t=PACK))
-        w1_raw[0, 1] = load_rows("w1_raw01", w1[PASS:K, 0:BANK])
-        w1_raw[1, 0] = load_rows("w1_raw10", w1[0:PASS, BANK:H])
-        load_scales_side_by_side(tab2_sc, tab2_scales)
-        tab2_w[0] = load_words("tab2_w0", tab2_words[0])
-        with nc.allow_non_contiguous_dma(reason="one bias value for each partition"):
-            nc.sync.dma_start(d_t[:], d.rearrange("(c p) -> p c", p=P))
-        tab2_w[1] = load_words("tab2_w1", tab2_words[1])
-        nc.sync.dma_start(w2_raw[:].bitcast(I32), w2_words.rearrange("a p c -> p a c").bitcast(I32))
-        load_scales_side_by_side(w2_sc_raw, w2_scales)
-        w1_raw[1, 1] = load_rows("w1_raw11", w1[PASS:K, BANK:H])
-        load_scales_side_by_side(w4_sc, w4_scales)
-        w3_raw[0] = load_rows("w3_raw0", w3[0:PASS, :])
-        w3_raw[1] = load_rows("w3_raw1", w3[PASS:H, :])
-        nc.sync.dma_start(w4_w[:].bitcast(I32), w4_words.rearrange("a p c i -> p a (c i)").bitcast(I32))
-
-        w1_q = {}
-
-        def bank(name, width, index):
-            return psum.tile([P, width], F32, name=name, tag="bank%d" % index)
-
-        def cast_w1(engine, b, a):
-            return interleave_permuted(engine, "w1_bf%d%d" % (b, a), w1_raw[b, a])
-
-        def gather_words(name, window, offsets, pieces):
-            n = offsets.shape[1] * 16
-            t = held(name, [P, n], U32)
-            step = n // pieces
-            for i in range(pieces):
-                nc.vector.tensor_copy(t[:, i * step:(i + 1) * step],
-                                      window[:].indirect(offsets[:, i * step // 16:(i + 1) * step // 16]))
+        def gather(name, dtype, window, offsets, tag=None):
+            t = tile(name, [P, offsets.shape[1] * 16], dtype, tag=tag)
+            nc.vector.tensor_copy(t[:], window.indirect(offsets[:]))
             return t
 
-        h = {}
-
-        def project_assemblies(b):
-            for t in range(PACK):
-                h[b, t] = held("h%d%d" % (b, t), [P, S], F32)
-                rows = slice(t * P, (t + 1) * P)
-                for half in range(S // BANK):
-                    cols = slice(half * BANK, (half + 1) * BANK)
-                    acc = bank("acc", BANK, 2 * t + half)
-                    for a in range(2):
-                        codes, scales = w1_q[b, a]
-                        nc.tensor.matmul_mx(out=acc[:], lhsT=codes[:, rows].bitcast(FP8X4), lhsT_scale=scales[:, rows],
-                                            rhs=v_w[a][:, cols].bitcast(FP8X4), rhs_scale=v_sc[4 * a:P, cols],
-                                            start=(a == 0), stop=(a == 1))
-                    nc.scalar.activation(h[b, t][:, cols], acc[:], IDENT, bias=b1_t[:, b, t:t + 1])
-
-        ident = held("ident", [P, P], F32)
-        make_identity(nc, ident[:])
-        b2_row = held("b2_row", [P, 2, PACK, P], F32)
-
-        def spread_bias():
+        def spread_b2():
+            rows = tile("b2_rows", [P, 2, PACK * P], F32)
             for b in range(2):
-                acc = bank("spread", BANK, 6 + b)
+                acc = bank("b2_spread", BANK, 6 + b)
                 for t in range(PACK):
-                    nc.tensor.transpose(acc[:, t * P:(t + 1) * P], b2_t[:, b, t:t + 1].to_broadcast([P, P]), ident[:])
-                nc.scalar.copy(b2_row[:, b, :, :].rearrange("p t m -> p (t m)"), acc[:])
+                    nc.tensor.transpose(acc[:, t * P:(t + 1) * P], b2_col[:, b, t:t + 1].to_broadcast([P, P]), ident[:])
+                nc.scalar.copy(rows[:, b, :], acc[:])
+            return rows
 
-        def project_components(b):
-            e_t = held("eT%d" % b, [P, M // P, PACK, P], F32, tag="eT", bufs=2)
-            e_bf = held("e_bf%d" % b, [P, M * PACK], BF16)
+        def project_assemblies(b, tag):
+            h = tile("h%d" % b, [P, PACK, S], F32, tag=tag)
+            for t in range(PACK):
+                rows = slice(t * P, (t + 1) * P)
+                for part in range(S // BANK):
+                    cols = slice(part * BANK, (part + 1) * BANK)
+                    acc = bank("h_sum", BANK, 2 * t + part)
+                    for a in range(2):
+                        codes, scales = w1_mx[b, a]
+                        nc.tensor.matmul_mx(out=acc[:], lhsT=codes[:, rows].bitcast(FP8X4), lhsT_scale=scales[:, rows],
+                                            rhs=v_words[a][:, cols].bitcast(FP8X4), rhs_scale=v_scales[4 * a:P, cols],
+                                            start=(a == 0), stop=(a == 1))
+                    nc.scalar.activation(h[:, t, cols], acc[:], IDENTITY, bias=b1_col[:, b, t:t + 1])
+            return h
+
+        def project_components(b, tag):
+            e_turned = tile("e_turned%d" % b, [P, M // P, PACK, P], F32, tag=tag)
+            e_bf16 = tile("e_bf16_%d" % b, [P, M * PACK], BF16)
             for c in range(M // P):
-                acc = bank("acc", BANK, c)
+                acc = bank("e_sum", BANK, c)
                 cols = slice(c * P, (c + 1) * P)
                 for a in range(2):
-                    nc.tensor.matmul_mx(out=acc[:], lhsT=v2_w[a][:, cols].bitcast(FP8X4), lhsT_scale=v2_sc[:, a, cols],
-                                        rhs=w2_raw[:, a, 2 * b * BANK:2 * (b + 1) * BANK].bitcast(FP4X4),
-                                        rhs_scale=w2_sc_raw[:, a * H + b * BANK:a * H + (b + 1) * BANK],
+                    nc.tensor.matmul_mx(out=acc[:], lhsT=v2_words[a][:, cols].bitcast(FP8X4),
+                                        lhsT_scale=v2_scales[a][:, cols],
+                                        rhs=w2_codes[:, a, 2 * b * BANK:2 * (b + 1) * BANK].bitcast(FP4X4),
+                                        rhs_scale=w2_plane[:, a * H + b * BANK:a * H + (b + 1) * BANK],
                                         start=(a == 0), stop=(a == 1))
-                nc.scalar.copy(e_t[:, c, :, :], acc[:].rearrange("m (p t) -> m t p", t=PACK))
-                turned = bank("turned", BANK, 4 + c)
+                nc.scalar.copy(e_turned[:, c, :, :], acc[:].rearrange("m (p t) -> m t p", t=PACK))
+            for c in range(M // P):
+                back = bank("e_back", BANK, 4 + c)
                 for t in range(PACK):
-                    nc.tensor.matmul(turned[:, t * P:(t + 1) * P], lhsT=b2_row[:, b, t, :], rhs=ident[:], is_transpose=True,
-                                     start=(t == 0), stop=False)
+                    nc.tensor.matmul(back[:, t * P:(t + 1) * P], lhsT=b2_rows[:, b, t * P:(t + 1) * P], rhs=ident[:],
+                                     is_transpose=True, start=(t == 0), stop=False)
                 for t in range(PACK):
-                    nc.tensor.matmul(turned[:, t * P:(t + 1) * P], lhsT=e_t[:, c, t, :], rhs=ident[:], is_transpose=True,
-                                     start=False, stop=(t == PACK - 1))
-                nc.scalar.copy(e_bf[:, c * P * PACK:(c + 1) * P * PACK].rearrange("p (m t) -> p m t", t=PACK),
-                               turned[:].rearrange("p (t m) -> p m t", t=PACK))
-            return e_bf
+                    nc.tensor.matmul(back[:, t * P:(t + 1) * P], lhsT=e_turned[:, c, t, :], rhs=ident[:],
+                                     is_transpose=True, start=False, stop=(t == PACK - 1))
+                nc.scalar.copy(e_bf16[:, c * PASS:(c + 1) * PASS].rearrange("p (m t) -> p m t", t=PACK),
+                               back[:].rearrange("p (t m) -> p m t", t=PACK))
+            return e_bf16
 
-        def fetch(engine, b, m0, width, dst):
-            x = held("x%d_%d" % (b, m0), [P, PACK, width], F32, tag="x")
+        def fetch(name, h, tag):
+            x = tile(name, [P, PACK, M], F32, tag=tag)
             for t in range(PACK):
-                nc.vector.tensor_copy(x[:, t, :], h[b, t][:].indirect(pos_t[:, m0 // 16:(m0 + width) // 16]))
-            copy(engine, dst.rearrange("p (c i j) -> p c j i", i=4, j=PACK), x[:].rearrange("p j (c i) -> p c j i", i=4))
+                nc.vector.tensor_copy(x[:, t, :], h[:, t, :].indirect(pos1_list[:]))
+            return x
 
-        def order(b, m0, width, x_bf, e_bf):
-            name = "%d_%d" % (b, m0)
-            hi = held("hi" + name, [P, width * PACK], BF16, tag="hi")
-            lo = held("lo" + name, [P, width * PACK], BF16, tag="lo")
-            e_part = e_bf[:, m0 * PACK:(m0 + width) * PACK]
-            nc.vector.tensor_tensor(hi[:], x_bf[:], e_part, ALU.max)
-            nc.vector.tensor_tensor(lo[:], x_bf[:], e_part, ALU.min)
-            return quantize("hi_q" + name, hi), quantize("lo_q" + name, lo)
+        def larger_and_smaller(name, x_bf16, e_bf16):
+            hi = tile(name + "_hi", list(x_bf16.shape), BF16, tag="hi")
+            lo = tile(name + "_lo", list(x_bf16.shape), BF16, tag="lo")
+            nc.vector.tensor_tensor(hi[:], x_bf16[:], e_bf16, ALU.max)
+            nc.vector.tensor_tensor(lo[:], x_bf16[:], e_bf16, ALU.min)
+            return quantize(name + "_hi", hi), quantize(name + "_lo", lo)
 
-        HALF = M // 2
-        y = {}
-
-        def score(b, side, half, operand, m0, start, stop):
-            codes, scales = operand
-            mc = slice(half * HALF - m0, (half + 1) * HALF - m0)
+        def score_pass(sums, weight, operand, cols, start, stop):
             for c in range(N // P):
-                if start:
-                    y[c, half] = bank("y", HALF, c + 4 * half)
-                cols = slice(c * P, (c + 1) * P)
-                if side == 0:
-                    w, ws = w3_q[b][0][:, cols], w3_q[b][1][:, cols]
-                else:
-                    w, ws = w4_w[:, b, cols], w4_sc[:, b * N + c * P:b * N + (c + 1) * P]
-                nc.tensor.matmul_mx(out=y[c, half][:], lhsT=w.bitcast(FP8X4), lhsT_scale=ws,
-                                    rhs=codes[:, mc].bitcast(FP8X4), rhs_scale=scales[:, mc], start=start, stop=stop)
+                rows = slice(c * P, (c + 1) * P)
+                nc.tensor.matmul_mx(out=sums[c][:], lhsT=weight[0][:, rows].bitcast(FP8X4), lhsT_scale=weight[1][:, rows],
+                                    rhs=operand[0][:, cols].bitcast(FP8X4), rhs_scale=operand[1][:, cols],
+                                    start=start, stop=stop)
 
-        def store(half, engines):
+        def store(half, sums, engines):
             for c in range(N // P):
-                res = held("res%d%d" % (c, half), [P, HALF], F32)
-                if engines[c] == "S":
-                    nc.scalar.activation(res[:], y[c, half][:], IDENT, bias=d_t[:, c:c + 1])
+                res = tile("res%d%d" % (half, c), [P, HALF], F32)
+                if engines[c] is nc.scalar:
+                    nc.scalar.activation(res[:], sums[c][:], IDENTITY, bias=d_col[:, c:c + 1])
                 else:
-                    nc.vector.tensor_scalar(res[:], y[c, half][:], d_t[:, c:c + 1], None, ALU.add)
+                    nc.vector.tensor_scalar(res[:], sums[c][:], d_col[:, c:c + 1], None, ALU.add)
                 nc.sync.dma_start(out[c * P:(c + 1) * P, half * HALF:(half + 1) * HALF], res[:])
 
-        v_w, v2_w, w3_q = {}, {}, {}
-        spread_bias()
-        v_sc = held("v_sc", [P, S], U8)
-        nc.vector.tensor_copy(v_sc[:], tab_sc[:].indirect(offs_t[:]))
-        v_w[0] = gather_words("v_w0", tab_w[0], offs_t, 1)
-        bf00 = cast_w1("S", 0, 0)
-        v_w[1] = gather_words("v_w1", tab_w[1], offs_t, 2)
-        w1_q[0, 0] = quantize("w1_q00", bf00)
-        bf01 = cast_w1("S", 0, 1)
-        w1_q[0, 1] = quantize("w1_q01", bf01)
-        v2_sc = held("v2_sc", [P, 2, M], U8)
-        for a in range(2):
-            nc.vector.tensor_copy(v2_sc[:, a, :], tab2_sc[:, a * T2:(a + 1) * T2].indirect(offs2_t[:]))
-        bf10 = cast_w1("S", 1, 0)
-        project_assemblies(0)
-        w1_q[1, 0] = quantize("w1_q10", bf10)
-        v2_w[0] = gather_words("v2_w0", tab2_w[0], offs2_t, 1)
-        v2_w[1] = gather_words("v2_w1", tab2_w[1], offs2_t, 1)
-        bf11 = cast_w1("S", 1, 1)
-        x0 = held("x_bf0", [P, M * PACK], BF16, tag="x_bf")
-        fetch("V", 0, 0, HALF, x0[:, 0:HALF * PACK])
-        w1_q[1, 1] = quantize("w1_q11", bf11)
-        fetch("V", 0, HALF, HALF, x0[:, HALF * PACK:M * PACK])
-        e0 = project_components(0)
-        project_assemblies(1)
-        bf30 = interleave("V", "w3_bf0", w3_raw[0][:], "wbf", 3)
-        w3_q[0] = quantize("w3_q0", bf30)
-        hi0, lo0 = order(0, 0, M, x0, e0)
-        e1 = project_components(1)
-        bf31 = interleave("S", "w3_bf1", w3_raw[1][:], "wbf", 3)
-        w3_q[1] = quantize("w3_q1", bf31)
-        score(0, 1, 0, lo0, 0, True, False)
-        score(0, 0, 0, hi0, 0, False, False)
-        x10 = held("x_bf10", [P, HALF * PACK], BF16, tag="x_bf")
-        fetch("V", 1, 0, HALF, x10[:])
-        hi10, lo10 = order(1, 0, HALF, x10, e1)
-        x11 = held("x_bf11", [P, HALF * PACK], BF16, tag="x_bf")
-        fetch("V", 1, HALF, HALF, x11[:])
-        score(0, 1, 1, lo0, 0, True, False)
-        score(0, 0, 1, hi0, 0, False, False)
-        score(1, 0, 0, hi10, 0, False, False)
-        score(1, 1, 0, lo10, 0, False, True)
-        store(0, "SSSS")
-        hi11, lo11 = order(1, HALF, HALF, x11, e1)
-        score(1, 0, 1, hi11, HALF, False, False)
-        score(1, 1, 1, lo11, HALF, False, True)
-        store(1, "SVSV")
+        ident = tile("ident", [P, P], F32)
+        make_identity(nc, ident[:])
+        b2_rows = spread_b2()
+
+        w1_mx = {}
+        v_scales = gather("v_scales", U8, tab_plane[:], offs_list)
+        v_words = [gather("v_words0", U32, tab_codes[0][:], offs_list)]
+        grouped = interleave_w1(0, 0)
+        v_words.append(gather("v_words1", U32, tab_codes[1][:], offs_list))
+        w1_mx[0, 0] = quantize("w1_00", grouped)
+        w1_mx[0, 1] = quantize("w1_01", interleave_w1(0, 1, "w1_bf16_01", 1))
+        v2_scales = [gather("v2_scales0", U8, tab2_plane[:, 0:T2], offs2_list),
+                     gather("v2_scales1", U8, tab2_plane[:, T2:2 * T2], offs2_list, "w1_bf16_01")]
+        w1_mx[1, 0] = quantize("w1_10", interleave_w1(1, 0))
+        h0 = project_assemblies(0, "w1_f32_10")
+        v2_words = [gather("v2_words%d" % a, U32, tab2_codes[a][:], offs2_list) for a in range(2)]
+
+        halves = [slice(0, HALF), slice(HALF, M)]
+        w4_mx = [(w4_codes[:, b, :], w4_plane[:, b * N:(b + 1) * N]) for b in range(2)]
+        x0 = interleave(nc.vector, "x0_bf16", fetch("x0", h0, "tab2_codes1")[:], "x_bf16", 2)
+        w1_mx[1, 1] = quantize("w1_11", interleave_w1(1, 1))
+        e0 = project_components(0, "w1_f32_11")
+        h1 = project_assemblies(1, "h1")
+        w3_mx = [quantize("w3_0", interleave(nc.vector, "w3_bf16_0", w3_f32[0][:], "weight_bf16", 3))]
+        hi0, lo0 = larger_and_smaller("block0", x0, e0[:])
+        x1 = fetch("x1", h1, "x1")
+        e1 = project_components(1, "e_turned1")
+        w3_mx.append(quantize("w3_1", interleave(nc.scalar, "w3_bf16_1", w3_f32[1][:], "w2_codes", 1)))
+        sums = [[bank("score", HALF, 4 * (1 - half) + c) for c in range(N // P)] for half in range(2)]
+        score_pass(sums[0], w4_mx[0], lo0, halves[0], True, False)
+        score_pass(sums[0], w3_mx[0], hi0, halves[0], False, False)
+        whole = slice(0, HALF)
+        x1_first = interleave(nc.vector, "x1_first", x1[:, :, halves[0]], "x_bf16", 2)
+        hi1, lo1 = larger_and_smaller("block1_first", x1_first, e1[:, 0:HALF * PACK])
+        x1_second = interleave(nc.vector, "x1_second", x1[:, :, halves[1]], "x_bf16", 2)
+        score_pass(sums[1], w4_mx[0], lo0, halves[1], True, False)
+        score_pass(sums[1], w3_mx[0], hi0, halves[1], False, False)
+        score_pass(sums[0], w3_mx[1], hi1, whole, False, False)
+        score_pass(sums[0], w4_mx[1], lo1, whole, False, True)
+        store(0, sums[0], [nc.scalar] * 4)
+        hi1, lo1 = larger_and_smaller("block1_second", x1_second, e1[:, HALF * PACK:M * PACK])
+        score_pass(sums[1], w3_mx[1], hi1, whole, False, False)
+        score_pass(sums[1], w4_mx[1], lo1, whole, False, True)
+        store(1, sums[1], [nc.scalar, nc.vector] * 2)

@@ -59,8 +59,8 @@ def tile_list_fit_margins_kernel(tc, tab_words, tab_scales, offs, pos1, tab2_wor
             for q in range(QUADRANTS):
                 nc.sync.dma_start(plane[32 * q:32 * q + 8, :].bitcast(I32), src[:, 4 * q:4 * q + 4, :].bitcast(I32))
 
-        def load_scales_side_by_side(plane, src):
-            for q in range(QUADRANTS):
+        def load_scales_side_by_side(plane, src, quadrants):
+            for q in quadrants:
                 nc.sync.dma_start(plane[32 * q:32 * q + 4, :].bitcast(I32).rearrange("i (a c) -> i a c", a=2),
                                   src[:, 4 * q:4 * q + 4, :].bitcast(I32).rearrange("a i c -> i a c"))
 
@@ -80,32 +80,34 @@ def tile_list_fit_margins_kernel(tc, tab_words, tab_scales, offs, pos1, tab2_wor
         w4_plane = zeroed_plane("w4_plane", 2 * N)
 
         tab_codes, tab2_codes, w1_f32, w3_f32 = {}, {}, {}, {}
-        load_scales_stacked(tab_plane, tab_scales)
+        tab_codes[0] = load_table_words("tab_codes0", tab_words[0])
         offs_list = load_list("offs_list", offs)
+        w1_f32[0, 0] = load_weight_pass("w1_f32_00", w1[0:PASS, 0:BANK])
+        load_scales_stacked(tab_plane, tab_scales)
+        tab_codes[1] = load_table_words("tab_codes1", tab_words[1])
+        w1_f32[0, 1] = load_weight_pass("w1_f32_01", w1[PASS:K, 0:BANK])
         b2_col = load_row_bias("b2_col", b2)
         offs2_list = load_list("offs2_list", offs2)
-        tab_codes[0] = load_table_words("tab_codes0", tab_words[0])
-        w1_f32[0, 0] = load_weight_pass("w1_f32_00", w1[0:PASS, 0:BANK])
-        pos1_list = load_list("pos1_list", pos1)
-        tab_codes[1] = load_table_words("tab_codes1", tab_words[1])
-        b1_col = load_row_bias("b1_col", b1)
-        w1_f32[0, 1] = load_weight_pass("w1_f32_01", w1[PASS:K, 0:BANK])
-        load_scales_side_by_side(tab2_plane, tab2_scales)
+        load_scales_side_by_side(tab2_plane, tab2_scales, (0, 1))
         w1_f32[1, 0] = load_weight_pass("w1_f32_10", w1[0:PASS, BANK:H], "w1_f32_10", 1)
+        load_scales_side_by_side(tab2_plane, tab2_scales, (2, 3))
+        tab2_codes[0] = load_table_words("tab2_codes0", tab2_words[0])
+        b1_col = load_row_bias("b1_col", b1)
+        pos1_list = load_list("pos1_list", pos1)
+        tab2_codes[1] = load_table_words("tab2_codes1", tab2_words[1])
+        w1_f32[1, 1] = load_weight_pass("w1_f32_11", w1[PASS:K, BANK:H], "w1_f32_11", 1)
+        w2_codes = tile("w2_codes", [P, 2, 2 * H], U8)
+        nc.sync.dma_start(w2_codes[:].bitcast(I32), w2_words.rearrange("a p c -> p a c").bitcast(I32))
+        load_scales_side_by_side(w2_plane, w2_scales, range(QUADRANTS))
+        w3_f32[0] = load_weight_pass("w3_f32_0", w3[0:PASS, :])
+        load_scales_side_by_side(w4_plane, w4_scales, (0, 1))
+        w3_f32[1] = load_weight_pass("w3_f32_1", w3[PASS:H, :])
+        load_scales_side_by_side(w4_plane, w4_scales, (2, 3))
+        w4_codes = tile("w4_codes", [P, 2, N], U32)
+        nc.sync.dma_start(w4_codes[:].bitcast(I32), w4_words.rearrange("a p c j -> p a (c j)").bitcast(I32))
         d_col = tile("d_col", [P, N // P], F32)
         with nc.allow_non_contiguous_dma(reason="one bias value for each partition"):
             nc.sync.dma_start(d_col[:], d.rearrange("(c p) -> p c", p=P))
-        tab2_codes[0] = load_table_words("tab2_codes0", tab2_words[0])
-        tab2_codes[1] = load_table_words("tab2_codes1", tab2_words[1])
-        w2_codes = tile("w2_codes", [P, 2, 2 * H], U8)
-        nc.sync.dma_start(w2_codes[:].bitcast(I32), w2_words.rearrange("a p c -> p a c").bitcast(I32))
-        load_scales_side_by_side(w2_plane, w2_scales)
-        w1_f32[1, 1] = load_weight_pass("w1_f32_11", w1[PASS:K, BANK:H], "w1_f32_11", 1)
-        w3_f32[0] = load_weight_pass("w3_f32_0", w3[0:PASS, :])
-        load_scales_side_by_side(w4_plane, w4_scales)
-        w3_f32[1] = load_weight_pass("w3_f32_1", w3[PASS:H, :])
-        w4_codes = tile("w4_codes", [P, 2, N], U32)
-        nc.sync.dma_start(w4_codes[:].bitcast(I32), w4_words.rearrange("a p c j -> p a (c j)").bitcast(I32))
 
         def copy(engine, dst, src):
             if engine is nc.scalar:
@@ -225,9 +227,9 @@ def tile_list_fit_margins_kernel(tc, tab_words, tab_scales, offs, pos1, tab2_wor
         grouped = interleave_w1(0, 0)
         v_words.append(gather("v_words1", U32, tab_codes[1][:], offs_list))
         w1_mx[0, 0] = quantize("w1_00", grouped)
-        w1_mx[0, 1] = quantize("w1_01", interleave_w1(0, 1, "w1_bf16_01", 1))
+        w1_mx[0, 1] = quantize("w1_01", interleave_w1(0, 1))
         v2_scales = [gather("v2_scales0", U8, tab2_plane[:, 0:T2], offs2_list),
-                     gather("v2_scales1", U8, tab2_plane[:, T2:2 * T2], offs2_list, "w1_bf16_01")]
+                     gather("v2_scales1", U8, tab2_plane[:, T2:2 * T2], offs2_list)]
         w1_mx[1, 0] = quantize("w1_10", interleave_w1(1, 0))
         h0 = project_assemblies(0, "w1_f32_10")
         v2_words = [gather("v2_words%d" % a, U32, tab2_codes[a][:], offs2_list) for a in range(2)]
@@ -242,7 +244,10 @@ def tile_list_fit_margins_kernel(tc, tab_words, tab_scales, offs, pos1, tab2_wor
         hi0, lo0 = larger_and_smaller("block0", x0, e0[:])
         x1 = fetch("x1", h1, "x1")
         e1 = project_components(1, "e_turned1")
-        w3_mx.append(quantize("w3_1", interleave(nc.scalar, "w3_bf16_1", w3_f32[1][:], "w2_codes", 1)))
+        w3_second = tile("w3_bf16_1", [P, BANK * PACK], BF16, tag="lo")
+        nc.gpsimd.tensor_scalar(w3_second[:].rearrange("p (c j) -> p c j", j=PACK), w3_f32[1][:].rearrange("p j c -> p c j"),
+                                1.0, 0.0, ALU.mult, ALU.add)
+        w3_mx.append(quantize("w3_1", w3_second))
         sums = [[bank("score", HALF, 4 * (1 - half) + c) for c in range(N // P)] for half in range(2)]
         score_pass(sums[0], w4_mx[0], lo0, halves[0], True, False)
         score_pass(sums[0], w3_mx[0], hi0, halves[0], False, False)

from contextlib import ExitStack

import concourse.mybir as mybir
from concourse.masks import make_identity

K, T, S, T2, M, H, N = 1024, 2048, 1024, 2048, 512, 1024, 512
FLOPS = 2 * K * H * S + 2 * K * H * M + 2 * 2 * H * N * M

F32 = mybir.dt.float32
BF16 = mybir.dt.bfloat16
I32 = mybir.dt.int32
U32 = mybir.dt.uint32
U16 = mybir.dt.uint16
U8 = mybir.dt.uint8
FP8X4 = mybir.dt.float8_e4m3fn_x4
FP4X4 = mybir.dt.float4_e2m1fn_x4
ALU = mybir.AluOpType
IDENTITY = mybir.ActivationFunctionType.Identity

P = 128
PACK = 4
PASS = P * PACK
BANK = 512
QUADRANTS = 4
RUN = 4
HALF = M // 2


def tile_list_fit_margins_kernel(tc, tab_words, tab_scales, offs, pos1, tab2_words, tab2_scales, offs2,
                                           w1, b1, w2_words, w2_scales, b2, w3, w4_words, w4_scales, d, out):
    nc = tc.nc
    with ExitStack() as ctx:
        lists = ctx.enter_context(tc.tile_pool(name="lists", bufs=1))
        sbuf = ctx.enter_context(tc.tile_pool(name="sbuf", bufs=1))
        psum = ctx.enter_context(tc.psum_pool(name="psum", bufs=1))

        def tile(name, shape, dtype, tag=None, bufs=1):
            return sbuf.tile(shape, dtype, name=name, tag=tag or name, bufs=bufs, align_bytes=64)

        def bank(name, width, index):
            return psum.tile([P, width], F32, name=name, tag="bank%d" % index)

        def load_list(name, src):
            t = lists.tile(list(src.shape), U16, name=name)
            nc.sync.dma_start(t[:], src)
            return t

        def load_table_words(name, src):
            t = tile(name, [P, src.shape[1]], U32)
            nc.sync.dma_start(t[:].bitcast(I32), src.rearrange("p c j -> p (c j)").bitcast(I32))
            return t

        def zeroed_plane(name, width):
            t = tile(name, [P, width], U8)
            nc.vector.memset(t[:].bitcast(I32), 0)
            return t

        def load_scales_stacked(plane, src):
            for q in range(QUADRANTS):
                nc.sync.dma_start(plane[32 * q:32 * q + 8, :].bitcast(I32), src[:, 4 * q:4 * q + 4, :].bitcast(I32))

        def load_scales_side_by_side(plane, src, quadrants):
            for q in quadrants:
                nc.sync.dma_start(plane[32 * q:32 * q + 4, :].bitcast(I32).rearrange("i (a c) -> i a c", a=2),
                                  src[:, 4 * q:4 * q + 4, :].bitcast(I32).rearrange("a i c -> i a c"))

        def load_weight_pass(name, rows, tag="weight_f32", bufs=2):
            t = tile(name, [P, PACK, BANK], F32, tag=tag, bufs=bufs)
            nc.sync.dma_start(t[:], rows.rearrange("(p j) c -> p j c", j=PACK))
            return t

        def load_row_bias(name, src):
            t = tile(name, [P, 2, PACK], F32)
            nc.sync.dma_start(t[:], src.rearrange("(b p t) -> p b t", b=2, t=PACK))
            return t

        tab_plane = zeroed_plane("tab_plane", T)
        tab2_plane = zeroed_plane("tab2_plane", 2 * T2)
        w2_plane = zeroed_plane("w2_plane", 2 * H)
        w4_plane = zeroed_plane("w4_plane", 2 * N)

        tab_codes, tab2_codes, w1_f32, w3_f32 = {}, {}, {}, {}
        tab_codes[0] = load_table_words("tab_codes0", tab_words[0])
        offs_list = load_list("offs_list", offs)
        w1_f32[0, 0] = load_weight_pass("w1_f32_00", w1[0:PASS, 0:BANK])
        load_scales_stacked(tab_plane, tab_scales)
        tab_codes[1] = load_table_words("tab_codes1", tab_words[1])
        w1_f32[0, 1] = load_weight_pass("w1_f32_01", w1[PASS:K, 0:BANK])
        b2_col = load_row_bias("b2_col", b2)
        offs2_list = load_list("offs2_list", offs2)
        load_scales_side_by_side(tab2_plane, tab2_scales, (0, 1))
        w1_f32[1, 0] = load_weight_pass("w1_f32_10", w1[0:PASS, BANK:H], "w1_f32_10", 1)
        load_scales_side_by_side(tab2_plane, tab2_scales, (2, 3))
        tab2_codes[0] = load_table_words("tab2_codes0", tab2_words[0])
        b1_col = load_row_bias("b1_col", b1)
        pos1_list = load_list("pos1_list", pos1)
        tab2_codes[1] = load_table_words("tab2_codes1", tab2_words[1])
        w1_f32[1, 1] = load_weight_pass("w1_f32_11", w1[PASS:K, BANK:H], "w1_f32_11", 1)
        w2_codes = tile("w2_codes", [P, 2, 2 * H], U8)
        nc.sync.dma_start(w2_codes[:].bitcast(I32), w2_words.rearrange("a p c -> p a c").bitcast(I32))
        load_scales_side_by_side(w2_plane, w2_scales, range(QUADRANTS))
        w3_f32[0] = load_weight_pass("w3_f32_0", w3[0:PASS, :])
        load_scales_side_by_side(w4_plane, w4_scales, (0, 1))
        w3_f32[1] = load_weight_pass("w3_f32_1", w3[PASS:H, :])
        load_scales_side_by_side(w4_plane, w4_scales, (2, 3))
        w4_codes = tile("w4_codes", [P, 2, N], U32)
        nc.sync.dma_start(w4_codes[:].bitcast(I32), w4_words.rearrange("a p c j -> p a (c j)").bitcast(I32))
        d_col = tile("d_col", [P, N // P], F32)
        with nc.allow_non_contiguous_dma(reason="one bias value for each partition"):
            nc.sync.dma_start(d_col[:], d.rearrange("(c p) -> p c", p=P))

        def copy(engine, dst, src):
            if engine is nc.scalar:
                nc.scalar.copy(dst, src)
            else:
                nc.vector.tensor_copy(dst, src)

        def interleave(engine, name, planes, tag, bufs):
            t = tile(name, [P, planes.shape[2] * PACK], BF16, tag=tag, bufs=bufs)
            copy(engine, t[:].rearrange("p (c i j) -> p c j i", i=RUN, j=PACK),
                 planes.rearrange("p j (c i) -> p c j i", i=RUN))
            return t

        def interleave_w1(b, a, tag="weight_bf16", bufs=3):
            t = tile("w1_bf16_%d%d" % (b, a), [P, BANK * PACK], BF16, tag=tag, bufs=bufs)
            nc.scalar.copy(t[:].rearrange("p (t m j) -> p m j t", t=PACK, j=PACK),
                           w1_f32[b, a][:].rearrange("p j (m t) -> p m j t", t=PACK))
            return t

        def quantize(name, grouped):
            width = grouped.shape[1] // PACK
            codes = tile(name + "_codes", [P, width], U32)
            scales = tile(name + "_scales", [P, width], U8)
            nc.vector.quantize_mx(out=codes[:].bitcast(FP8X4), scales=scales[:], in_=grouped[:])
            return codes, scales

        def gather(name, dtype, window, offsets, tag=None):
            t = tile(name, [P, offsets.shape[1] * 16], dtype, tag=tag)
            nc.vector.tensor_copy(t[:], window.indirect(offsets[:]))
            return t

        def spread_b2():
            rows = tile("b2_rows", [P, 2, PACK * P], F32)
            for b in range(2):
                acc = bank("b2_spread", BANK, 6 + b)
                for t in range(PACK):
                    nc.tensor.transpose(acc[:, t * P:(t + 1) * P], b2_col[:, b, t:t + 1].to_broadcast([P, P]), ident[:])
                nc.scalar.copy(rows[:, b, :], acc[:])
            return rows

        def project_assemblies(b, tag):
            h = tile("h%d" % b, [P, PACK, S], F32, tag=tag)
            for t in range(PACK):
                rows = slice(t * P, (t + 1) * P)
                for part in range(S // BANK):
                    cols = slice(part * BANK, (part + 1) * BANK)
                    acc = bank("h_sum", BANK, 2 * t + part)
                    for a in range(2):
                        codes, scales = w1_mx[b, a]
                        nc.tensor.matmul_mx(out=acc[:], lhsT=codes[:, rows].bitcast(FP8X4), lhsT_scale=scales[:, rows],
                                            rhs=v_words[a][:, cols].bitcast(FP8X4), rhs_scale=v_scales[4 * a:P, cols],
                                            start=(a == 0), stop=(a == 1))
                    nc.scalar.activation(h[:, t, cols], acc[:], IDENTITY, bias=b1_col[:, b, t:t + 1])
            return h

        def project_components(b, tag):
            e_turned = tile("e_turned%d" % b, [P, M // P, PACK, P], F32, tag=tag)
            e_bf16 = tile("e_bf16_%d" % b, [P, M * PACK], BF16)
            for c in range(M // P):
                acc = bank("e_sum", BANK, c)
                cols = slice(c * P, (c + 1) * P)
                for a in range(2):
                    nc.tensor.matmul_mx(out=acc[:], lhsT=v2_words[a][:, cols].bitcast(FP8X4),
                                        lhsT_scale=v2_scales[a][:, cols],
                                        rhs=w2_codes[:, a, 2 * b * BANK:2 * (b + 1) * BANK].bitcast(FP4X4),
                                        rhs_scale=w2_plane[:, a * H + b * BANK:a * H + (b + 1) * BANK],
                                        start=(a == 0), stop=(a == 1))
                nc.scalar.copy(e_turned[:, c, :, :], acc[:].rearrange("m (p t) -> m t p", t=PACK))
            for c in range(M // P):
                back = bank("e_back", BANK, 4 + c)
                for t in range(PACK):
                    nc.tensor.matmul(back[:, t * P:(t + 1) * P], lhsT=b2_rows[:, b, t * P:(t + 1) * P], rhs=ident[:],
                                     is_transpose=True, start=(t == 0), stop=False)
                for t in range(PACK):
                    nc.tensor.matmul(back[:, t * P:(t + 1) * P], lhsT=e_turned[:, c, t, :], rhs=ident[:],
                                     is_transpose=True, start=False, stop=(t == PACK - 1))
                nc.scalar.copy(e_bf16[:, c * PASS:(c + 1) * PASS].rearrange("p (m t) -> p m t", t=PACK),
                               back[:].rearrange("p (t m) -> p m t", t=PACK))
            return e_bf16

        def fetch(name, h, tag):
            x = tile(name, [P, PACK, M], F32, tag=tag)
            for t in range(PACK):
                nc.vector.tensor_copy(x[:, t, :], h[:, t, :].indirect(pos1_list[:]))
            return x

        def larger_and_smaller(name, x_bf16, e_bf16):
            hi = tile(name + "_hi", list(x_bf16.shape), BF16, tag="hi")
            lo = tile(name + "_lo", list(x_bf16.shape), BF16, tag="lo")
            nc.vector.tensor_tensor(hi[:], x_bf16[:], e_bf16, ALU.max)
            nc.vector.tensor_tensor(lo[:], x_bf16[:], e_bf16, ALU.min)
            return quantize(name + "_hi", hi), quantize(name + "_lo", lo)

        def score_pass(sums, weight, operand, cols, start, stop):
            for c in range(N // P):
                rows = slice(c * P, (c + 1) * P)
                nc.tensor.matmul_mx(out=sums[c][:], lhsT=weight[0][:, rows].bitcast(FP8X4), lhsT_scale=weight[1][:, rows],
                                    rhs=operand[0][:, cols].bitcast(FP8X4), rhs_scale=operand[1][:, cols],
                                    start=start, stop=stop)

        def store(half, sums, engines):
            for c in range(N // P):
                res = tile("res%d%d" % (half, c), [P, HALF], F32)
                if engines[c] is nc.scalar:
                    nc.scalar.activation(res[:], sums[c][:], IDENTITY, bias=d_col[:, c:c + 1])
                else:
                    nc.vector.tensor_scalar(res[:], sums[c][:], d_col[:, c:c + 1], None, ALU.add)
                nc.sync.dma_start(out[c * P:(c + 1) * P, half * HALF:(half + 1) * HALF], res[:])

        ident = tile("ident", [P, P], F32)
        make_identity(nc, ident[:])
        b2_rows = spread_b2()

        w1_mx = {}
        v_scales = gather("v_scales", U8, tab_plane[:], offs_list)
        v_words = [gather("v_words0", U32, tab_codes[0][:], offs_list)]
        grouped = interleave_w1(0, 0)
        v_words.append(gather("v_words1", U32, tab_codes[1][:], offs_list))
        w1_mx[0, 0] = quantize("w1_00", grouped)
        w1_mx[0, 1] = quantize("w1_01", interleave_w1(0, 1))
        v2_scales = [gather("v2_scales0", U8, tab2_plane[:, 0:T2], offs2_list),
                     gather("v2_scales1", U8, tab2_plane[:, T2:2 * T2], offs2_list)]
        w1_mx[1, 0] = quantize("w1_10", interleave_w1(1, 0))
        h0 = project_assemblies(0, "w1_f32_10")
        v2_words = [gather("v2_words%d" % a, U32, tab2_codes[a][:], offs2_list) for a in range(2)]

        halves = [slice(0, HALF), slice(HALF, M)]
        w4_mx = [(w4_codes[:, b, :], w4_plane[:, b * N:(b + 1) * N]) for b in range(2)]
        x0 = interleave(nc.vector, "x0_bf16", fetch("x0", h0, "tab2_codes1")[:], "x_bf16", 2)
        w1_mx[1, 1] = quantize("w1_11", interleave_w1(1, 1))
        e0 = project_components(0, "w1_f32_11")
        h1 = project_assemblies(1, "h1")
        w3_mx = [quantize("w3_0", interleave(nc.vector, "w3_bf16_0", w3_f32[0][:], "weight_bf16", 3))]
        hi0, lo0 = larger_and_smaller("block0", x0, e0[:])
        x1 = fetch("x1", h1, "x1")
        e1 = project_components(1, "e_turned1")
        w3_second = tile("w3_bf16_1", [P, BANK * PACK], BF16, tag="lo")
        nc.gpsimd.tensor_scalar(w3_second[:].rearrange("p (c j) -> p c j", j=PACK), w3_f32[1][:].rearrange("p j c -> p c j"),
                                1.0, 0.0, ALU.mult, ALU.add)
        w3_mx.append(quantize("w3_1", w3_second))
        sums = [[bank("score", HALF, 4 * (1 - half) + c) for c in range(N // P)] for half in range(2)]
        score_pass(sums[0], w4_mx[0], lo0, halves[0], True, False)
        score_pass(sums[0], w3_mx[0], hi0, halves[0], False, False)
        whole = slice(0, HALF)
        x1_first = interleave(nc.vector, "x1_first", x1[:, :, halves[0]], "x_bf16", 2)
        hi1, lo1 = larger_and_smaller("block1_first", x1_first, e1[:, 0:HALF * PACK])
        x1_second = interleave(nc.vector, "x1_second", x1[:, :, halves[1]], "x_bf16", 2)
        score_pass(sums[1], w4_mx[0], lo0, halves[1], True, False)
        score_pass(sums[1], w3_mx[0], hi0, halves[1], False, False)
        score_pass(sums[0], w3_mx[1], hi1, whole, False, False)
        score_pass(sums[0], w4_mx[1], lo1, whole, False, True)
        store(0, sums[0], [nc.scalar] * 4)
        hi1, lo1 = larger_and_smaller("block1_second", x1_second, e1[:, HALF * PACK:M * PACK])
        score_pass(sums[1], w3_mx[1], hi1, whole, False, False)
        score_pass(sums[1], w4_mx[1], lo1, whole, False, True)
        store(1, sums[1], [nc.scalar, nc.vector] * 2)
